import numpy as np
CORES = [231,239,247,255,103,111,119,127]
N = 8
MB, TK = 4, 32
def setup_inputs(rng):
    return {"x": rng.standard_normal((N, MB, 128, TK), dtype=np.float32), "w": (rng.standard_normal((N, 128, 128), dtype=np.float32) / 8)}
def reference(x, w):
    def run(a, W, order):
        for s in order:
            a = np.maximum(np.einsum("kf,bkn->bfn", W[s].astype(np.float64), a), 0.0)
        return a
    dt = np.float32 if x.dtype != np.float64 else np.float64
    y = np.full(x.shape, np.nan, dt)
    y[N - 1] = run(x[0].astype(np.float64), w, range(N)).astype(dt)
    return {"y": y}

@@ -1,0 +1,81 @@
+from concourse.mybir import AluOpType
+
+PLAN = ((0, (0, 1, 2)), (7, (3, 4, 5, 6, 7)))
+H = 2
+HC = 128 // H
+NMAX = max(len(p[1]) for p in PLAN)
+
+SCRATCH = {
+    "wd": ("dram", [128, 128], "float32"),
+    "wb": ("sbuf", [128, NMAX * 128], "float32"),
+    "ac": ("sbuf", [128, (NMAX + 1) * 128], "float32"),
+    "zz": ("sbuf", [128, HC], "float32"),
+}
+for _b in range(8):
+    SCRATCH["ps%d" % _b] = ("psum", [128, 512], "float32")
+
+SEMAPHORES = ["ld", "sent", "ain", "zs", "st"] + ["w%d" % l for l in range(8)] \
+    + ["xin%d" % h for h in range(H)] + ["mm%d" % h for h in range(H)] + ["rl%d" % h for h in range(H)]
+
+
+def rank_program(g, core, T, topo):
+    r = T.rank_of(core)
+    if r is None:
+        return
+    sem = T.sem
+    where = {}
+    for si, (srank, layers) in enumerate(PLAN):
+        for slot, l in enumerate(layers):
+            where[l] = (si, slot)
+    si, slot = where[r]
+    srank, layers = PLAN[si]
+
+    if srank != r:
+        g.sync.dma_start(T.wd[:], T.w[:]).then_inc(sem.ld, 16)
+        g.wait_ge(sem.ld, 16)
+        rid, pid = topo.addr(T.cores[srank], core)
+        g.remote_dma(out_ap=T.wb[:, slot * 128:(slot + 1) * 128], in_ap=T.wd[:], remote_sem=sem["w%d" % r],
+                     local_sem=sem.sent, pid=pid, routing_id=rid, dma_engine_mask=0xFF)
+        g.wait_ge(sem.sent, 8)
+        return
+
+    n = len(layers)
+    first, last = si == 0, si == len(PLAN) - 1
+    g.vector.memset(T.zz[:], 0.0).then_inc(sem.zs, 1)
+    g.vector.wait_ge(sem.zs, 1)
+    g.sync.dma_start(T.wb[:, slot * 128:(slot + 1) * 128], T.w[:]).then_inc(sem["w%d" % r], 16)
+    if first:
+        for m in range(4):
+            q = g.scalar if m % 2 == 0 else g.sync
+            q.dma_start(T.ac[:, m * 32:(m + 1) * 32], T.x[m]).then_inc(sem["xin%d" % (m * H // 4)], 16)
+
+    for i, l in enumerate(layers):
+        g.tensor.wait_ge(sem["w%d" % l], 16 if l == r else 8)
+        if i == 0 and not first:
+            g.tensor.wait_ge(sem.ain, 8)
+        for h in range(H):
+            if i > 0:
+                g.tensor.wait_ge(sem["rl%d" % h], i)
+            elif first:
+                g.tensor.wait_ge(sem["xin%d" % h], 16 * (4 // H))
+            ps = T["ps%d" % ((i * H + h) % 8)]
+            c = i * 128 + h * HC
+            g.tensor.matmul(ps[:, 0:HC], T.wb[:, i * 128:(i + 1) * 128], T.ac[:, c:c + HC], True, True) \
+                .then_inc(sem["mm%d" % h], 1)
+            g.vector.wait_ge(sem["mm%d" % h], i + 1)
+            g.vector.tensor_tensor(T.ac[:, c + 128:c + 128 + HC], ps[:, 0:HC], T.zz[:], AluOpType.max) \
+                .then_inc(sem["rl%d" % h], 1)
+
+    if not last:
+        for h in range(H):
+            g.wait_ge(sem["rl%d" % h], n)
+        rid, pid = topo.addr(T.cores[PLAN[si + 1][0]], core)
+        g.remote_dma(out_ap=T.ac[:, 0:128], in_ap=T.ac[:, n * 128:(n + 1) * 128], remote_sem=sem.ain,
+                     local_sem=sem.sent, pid=pid, routing_id=rid, dma_engine_mask=0xFF)
+        g.wait_ge(sem.sent, 8)
+    else:
+        for m in range(4):
+            q = g.scalar if m % 2 == 0 else g.sync
+            q.wait_ge(sem["rl%d" % (m * H // 4)], n)
+            q.dma_start(T.y[m], T.ac[:, n * 128 + m * 32:n * 128 + (m + 1) * 32]).then_inc(sem.st, 16)
+        g.wait_ge(sem.st, 64)

@@ -1,6 +1,6 @@
 from concourse.mybir import AluOpType
 
-PLAN = ((0, (0, 1, 2)), (7, (3, 4, 5, 6, 7)))
+PLAN = ((0, (0,)), (7, (1, 2, 3, 4, 5, 6, 7)))
 H = 2
 HC = 128 // H
 NMAX = max(len(p[1]) for p in PLAN)
@@ -14,29 +14,48 @@ SCRATCH = {
 for _b in range(8):
     SCRATCH["ps%d" % _b] = ("psum", [128, 512], "float32")
 
-SEMAPHORES = ["ld", "sent", "ain", "zs", "st"] + ["w%d" % l for l in range(8)] \
+SEMAPHORES = ["ld", "sent", "ain", "rin", "zs", "st"] + ["w%d" % l for l in range(8)] \
     + ["xin%d" % h for h in range(H)] + ["mm%d" % h for h in range(H)] + ["rl%d" % h for h in range(H)]
 
 
 def rank_program(g, core, T, topo):
-    r = T.rank_of(core)
-    if r is None:
-        return
     sem = T.sem
     where = {}
     for si, (srank, layers) in enumerate(PLAN):
         for slot, l in enumerate(layers):
             where[l] = (si, slot)
+    relay = {3: T.cores[3] - 4, 5: T.cores[5] - 4, 4: T.cores[6] - 1}
+
+    def send_w(l, src_core):
+        s, slot = where[l]
+        rid, pid = topo.addr(T.cores[PLAN[s][0]], src_core)
+        g.remote_dma(out_ap=T.wb[:, slot * 128:(slot + 1) * 128], in_ap=T.wd[:], remote_sem=sem["w%d" % l],
+                     local_sem=sem.sent, pid=pid, routing_id=rid, dma_engine_mask=0xFF)
+        g.wait_ge(sem.sent, 8)
+
+    r = T.rank_of(core)
+    if r is None:
+        for l, hc in relay.items():
+            if hc == core:
+                k = 16 if topo.mask(T.cores[l], core) == 0xFFFF else 8
+                g.wait_ge(sem.rin, k)
+                send_w(l, core)
+        return
+
     si, slot = where[r]
     srank, layers = PLAN[si]
 
     if srank != r:
         g.sync.dma_start(T.wd[:], T.w[:]).then_inc(sem.ld, 16)
         g.wait_ge(sem.ld, 16)
-        rid, pid = topo.addr(T.cores[srank], core)
-        g.remote_dma(out_ap=T.wb[:, slot * 128:(slot + 1) * 128], in_ap=T.wd[:], remote_sem=sem["w%d" % r],
-                     local_sem=sem.sent, pid=pid, routing_id=rid, dma_engine_mask=0xFF)
-        g.wait_ge(sem.sent, 8)
+        if r in relay:
+            mk = topo.mask(core, relay[r])
+            rid, pid = topo.addr(relay[r], core)
+            g.remote_dma(out_ap=T.wd[:], in_ap=T.wd[:], remote_sem=sem.rin, local_sem=sem.sent, pid=pid,
+                         routing_id=rid, dma_engine_mask=mk)
+            g.wait_ge(sem.sent, 16 if mk == 0xFFFF else 8)
+        else:
+            send_w(r, core)
         return
 
     n = len(layers)

from concourse.mybir import AluOpType

PLAN = ((0, (0,)), (7, (1, 2, 3, 4, 5, 6, 7)))
H = 2
HC = 128 // H
NMAX = max(len(p[1]) for p in PLAN)

SCRATCH = {
    "wd": ("dram", [128, 128], "float32"),
    "wb": ("sbuf", [128, NMAX * 128], "float32"),
    "ac": ("sbuf", [128, (NMAX + 1) * 128], "float32"),
    "zz": ("sbuf", [128, HC], "float32"),
}
for _b in range(8):
    SCRATCH["ps%d" % _b] = ("psum", [128, 512], "float32")

SEMAPHORES = ["ld", "sent", "ain", "rin", "zs", "st"] + ["w%d" % l for l in range(8)] \
    + ["xin%d" % h for h in range(H)] + ["mm%d" % h for h in range(H)] + ["rl%d" % h for h in range(H)]


def rank_program(g, core, T, topo):
    sem = T.sem
    where = {}
    for si, (srank, layers) in enumerate(PLAN):
        for slot, l in enumerate(layers):
            where[l] = (si, slot)
    relay = {3: T.cores[3] - 4, 5: T.cores[5] - 4, 4: T.cores[6] - 1}

    def send_w(l, src_core):
        s, slot = where[l]
        rid, pid = topo.addr(T.cores[PLAN[s][0]], src_core)
        g.remote_dma(out_ap=T.wb[:, slot * 128:(slot + 1) * 128], in_ap=T.wd[:], remote_sem=sem["w%d" % l],
                     local_sem=sem.sent, pid=pid, routing_id=rid, dma_engine_mask=0xFF)
        g.wait_ge(sem.sent, 8)

    r = T.rank_of(core)
    if r is None:
        for l, hc in relay.items():
            if hc == core:
                k = 16 if topo.mask(T.cores[l], core) == 0xFFFF else 8
                g.wait_ge(sem.rin, k)
                send_w(l, core)
        return

    si, slot = where[r]
    srank, layers = PLAN[si]

    if srank != r:
        g.sync.dma_start(T.wd[:], T.w[:]).then_inc(sem.ld, 16)
        g.wait_ge(sem.ld, 16)
        if r in relay:
            mk = topo.mask(core, relay[r])
            rid, pid = topo.addr(relay[r], core)
            g.remote_dma(out_ap=T.wd[:], in_ap=T.wd[:], remote_sem=sem.rin, local_sem=sem.sent, pid=pid,
                         routing_id=rid, dma_engine_mask=mk)
            g.wait_ge(sem.sent, 16 if mk == 0xFFFF else 8)
        else:
            send_w(r, core)
        return

    n = len(layers)
    first, last = si == 0, si == len(PLAN) - 1
    g.vector.memset(T.zz[:], 0.0).then_inc(sem.zs, 1)
    g.vector.wait_ge(sem.zs, 1)
    g.sync.dma_start(T.wb[:, slot * 128:(slot + 1) * 128], T.w[:]).then_inc(sem["w%d" % r], 16)
    if first:
        for m in range(4):
            q = g.scalar if m % 2 == 0 else g.sync
            q.dma_start(T.ac[:, m * 32:(m + 1) * 32], T.x[m]).then_inc(sem["xin%d" % (m * H // 4)], 16)

    for i, l in enumerate(layers):
        g.tensor.wait_ge(sem["w%d" % l], 16 if l == r else 8)
        if i == 0 and not first:
            g.tensor.wait_ge(sem.ain, 8)
        for h in range(H):
            if i > 0:
                g.tensor.wait_ge(sem["rl%d" % h], i)
            elif first:
                g.tensor.wait_ge(sem["xin%d" % h], 16 * (4 // H))
            ps = T["ps%d" % ((i * H + h) % 8)]
            c = i * 128 + h * HC
            g.tensor.matmul(ps[:, 0:HC], T.wb[:, i * 128:(i + 1) * 128], T.ac[:, c:c + HC], True, True) \
                .then_inc(sem["mm%d" % h], 1)
            g.vector.wait_ge(sem["mm%d" % h], i + 1)
            g.vector.tensor_tensor(T.ac[:, c + 128:c + 128 + HC], ps[:, 0:HC], T.zz[:], AluOpType.max) \
                .then_inc(sem["rl%d" % h], 1)

    if not last:
        for h in range(H):
            g.wait_ge(sem["rl%d" % h], n)
        rid, pid = topo.addr(T.cores[PLAN[si + 1][0]], core)
        g.remote_dma(out_ap=T.ac[:, 0:128], in_ap=T.ac[:, n * 128:(n + 1) * 128], remote_sem=sem.ain,
                     local_sem=sem.sent, pid=pid, routing_id=rid, dma_engine_mask=0xFF)
        g.wait_ge(sem.sent, 8)
    else:
        for m in range(4):
            q = g.scalar if m % 2 == 0 else g.sync
            q.wait_ge(sem["rl%d" % (m * H // 4)], n)
            q.dma_start(T.y[m], T.ac[:, n * 128 + m * 32:n * 128 + (m + 1) * 32]).then_inc(sem.st, 16)
        g.wait_ge(sem.st, 64)
